import numpy as np, ml_dtypes
CORES = [89,94,345,350]
N = 4
import mx_ref
NC, WT = 256, 1
LR = np.float32(2.0 ** -4)
BF = ml_dtypes.bfloat16
def cut(t, i, w=512):
    return t[:, w * i:w * i + w]
def tile(rs):
    return np.stack(rs, axis=2).reshape(128, -1).astype(BF)
def pick(b):
    s = np.zeros((128, 128, 4), np.float32)
    s[np.arange(128), np.arange(128), b] = 1.0
    return mx_ref.quantize(s.reshape(128, 512).astype(BF))
def pk(c, s, i=0):
    return (np.ascontiguousarray(c[:, 512 * i:512 * i + 512]), mx_ref.live(s[:, 128 * i:128 * i + 128]))
def inputs(rng, e, E):
    def f(*shape):
        v = (rng.standard_normal(shape, dtype=np.float32) * np.exp2(rng.integers(-2, 3, shape[:-1] + (1,)))).astype(BF)
        return mx_ref.spread((v.astype(np.float32) * np.exp2(rng.integers(-E, E + 1, shape[:-2] + (1, 1))).astype(np.float32)).astype(BF), rng, e)
    def packed(k):
        c = np.zeros((N, 128, k * 512), np.uint8); s = np.zeros((N, 128, k * 128), np.uint8)
        for r in range(N):
            for i in range(k):
                a, b = mx_ref.quantize(f(128, 512)); c[r][:, 512 * i:512 * i + 512] = a; s[r][:, 128 * i:128 * i + 128] = mx_ref.plane(b, rng)
        return c, s
    d = {}
    d["wc"], d["ws"] = packed(WT)
    d["gr"] = f(N, 128, WT * 512)
    d["x"] = f(N, 128, 4 * NC)
    return d
def setup_inputs(rng):
    return inputs(rng, 0, 0)
def setup_inputs_blocks(rng):
    return inputs(rng, 2, 0)
def setup_inputs_wide(rng):
    return inputs(rng, 0, 4)
def setup_inputs_faint(rng):
    d = setup_inputs(rng); d["gr"] = mx_ref.flush((d["gr"].astype(np.float32) * np.float32(2.0 ** -12)).astype(BF))
    return d
def reference(wc, ws, gr, x):
    S = [pick(t) for t in range(4)]
    H = [mx_ref.quantize(tile([mx_ref.matmul(S[t], pk(wc[j], ws[j], i)) - cut(gr[j], i).astype(np.float32)[:, t::4] * LR for t in range(4)])) for j in range(N) for i in range(WT)]
    y = np.zeros((N, 128, N * WT * NC), np.float32)
    for r in range(N):
        X = mx_ref.quantize(x[r])
        for b in range(N * WT):
            y[r][:, NC * b:NC * b + NC] = mx_ref.matmul(H[b], X)
    return {"y": y}

@@ -1,0 +1,191 @@
+from concourse.bass import DstId, RemoteDMATransfer
+from concourse.mybir import dt, AluOpType, ActivationFunctionType
+
+N, NC, W = 4, 256, 128
+HOSTS, PER_HOST, PER_CHIP = 4, 128, 8
+
+SCRATCH = {
+    "e": ("sbuf", [128, 516], "bfloat16"),
+    "one": ("sbuf", [128, 128], "bfloat16"),
+    "g": ("sbuf", [128, 512], "bfloat16"),
+    "v": ("sbuf", [128, 512], "bfloat16"),
+    "xt": ("sbuf", [128, 1024], "bfloat16"),
+    "xc": ("sbuf", [128, 256], "float8_e4m3fn_x4"),
+    "xs": ("sbuf", [128, 256], "uint8"),
+    "kc": ("sbuf", [128, 512], "float8_e4m3fn_x4"),
+    "ks": ("sbuf", [128, 512], "uint8"),
+    "lc": ("sbuf", [128, 128], "float8_e4m3fn_x4"),
+    "ls": ("sbuf", [128, 128], "uint8"),
+    "o": ("sbuf", [128, N * NC], "float32"),
+    "pd": ("psum", [128, 2048], "float32"),
+    "py": ("psum", [128, 2048], "float32"),
+}
+for _j in range(N):
+    SCRATCH["c%d" % _j] = ("sbuf", [128, 128], "float8_e4m3fn_x4")
+    SCRATCH["s%d" % _j] = ("sbuf", [128, 128], "uint8")
+SEMAPHORES = ["seed", "ident", "sq", "ldw", "ldg", "ldx", "gs", "d0", "d1", "d2", "d3", "sub", "vq", "xq",
+              "arr0", "arr1", "arr2", "arr3", "rin", "sent", "m0", "m1", "m2", "m3", "n2", "n3",
+              "k0", "k1", "k2", "k3", "l2", "l3", "st", "sz"]
+
+CODES_A, CODES_B, PLANE = "codes_a", "codes_b", "plane"
+SPLIT = 64
+
+
+def engines(topo, src, dst):
+    m = topo.mask(src, dst)
+    return [i for i in range(16) if (m >> i) & 1]
+
+
+def bits(es):
+    return sum(1 << i for i in es)
+
+
+def to(topo, dst, src):
+    rid, pid = topo.addr(dst, src)
+    return DstId(rid=rid, pnc=pid)
+
+
+def near(topo, a, b):
+    return topo.host(a) == topo.host(b) and topo.chip(a) == topo.chip(b)
+
+
+def relays(topo, src, dst):
+    cable, switch = [], []
+    for c in range(HOSTS * PER_HOST):
+        if (topo.host(c) not in (topo.host(src), topo.host(dst)) and topo.chip(c) == topo.chip(src)
+                and topo.die(c) == topo.die(src) and topo.may_write(src, c) and topo.may_write(c, dst)):
+            (switch if topo.rack(topo.host(c)) == topo.rack(topo.host(src)) else cable).append(c)
+    return {CODES_A: cable[1], CODES_B: switch[0], PLANE: switch[-1]}
+
+
+def view(T, j, piece):
+    if piece == PLANE:
+        return T["s%d" % j][:]
+    a, b = {CODES_A: (0, SPLIT), CODES_B: (SPLIT, W)}.get(piece, (0, W))
+    return T["c%d" % j][:, a:b].bitcast(dt.uint8)
+
+
+def rank_program(g, core, T, topo):
+    rank = T.rank_of(core)
+    sem = T.sem
+    far = {j: [d for d in T.cores if not near(topo, d, c)] for j, c in enumerate(T.cores)}
+    way = {j: relays(topo, c, far[j][0]) for j, c in enumerate(T.cores)}
+
+    if rank is None:
+        for j in range(N):
+            for piece in (CODES_A, CODES_B, PLANE):
+                if way[j][piece] == core:
+                    src = T.cores[j]
+                    es = engines(topo, core, far[j][0])
+                    g.wait_ge(sem.rin, len(first_mask(topo, src, core, piece)))
+                    v = view(T, j, piece)
+                    g.remote_dma_fused([RemoteDMATransfer(dst_ids=[to(topo, d, core) for d in far[j]], dma_engine_mask=bits(es),
+                                                          remote_sem=sem["arr%d" % j], srcs=[v], dsts=[v for d in far[j]])],
+                                       local_sem=sem.sent)
+                    g.wait_ge(sem.sent, len(es))
+        return
+
+    mate = [j for j, c in enumerate(T.cores) if c != core and near(topo, c, core)][0]
+    away = [j for j, c in enumerate(T.cores) if not near(topo, c, core)]
+
+    g.sync.dma_start(T.lc[:].bitcast(dt.uint8), T.wc[:]).then_inc(sem.ldw, 16)
+    g.sync.dma_start(T.ls[:], T.ws[:]).then_inc(sem.ldw, 16)
+    g.scalar.dma_start(T.g[:], T.gr[:]).then_inc(sem.ldg, 16)
+    g.scalar.dma_start(T.xt[:], T.x[:]).then_inc(sem.ldx, 16)
+
+    g.vector.memset(T.e[:], 0.0).then_inc(sem.seed, 1)
+    g.vector.memset(T.one[:], 1.0).then_inc(sem.seed, 1)
+    g.wait_ge(sem.seed, 2)
+    g.affine_select(T.e[:, 3:515:4], T.one[:], [[-1, 128]], AluOpType.is_equal, 0.0, 0, 1).then_inc(sem.ident, 1)
+    g.vector.wait_ge(sem.ident, 1)
+    for b in range(4):
+        g.vector.quantize_mx(T.kc[:, W * b:W * b + W], T.ks[:, W * b:W * b + W], T.e[:, 3 - b:515 - b]).then_inc(sem.sq, 1)
+    g.vector.wait_ge(sem.ldg, 16)
+    g.vector.tensor_scalar(T.g[:], T.g[:], 2.0 ** -4, None, AluOpType.mult).then_inc(sem.gs, 1)
+
+    g.tensor.wait_ge(sem.sq, 4)
+    g.tensor.wait_ge(sem.ldw, 32)
+    for b in range(4):
+        g.tensor.matmul_mx(T.pd[:, 512 * b:512 * b + W], T.kc[:, W * b:W * b + W], T.ks[:, W * b:W * b + W], T.lc[:], T.ls[:],
+                           True, True).then_inc(sem["d%d" % b], 1)
+
+    g.vector.wait_ge(sem.gs, 1)
+    for b in range(4):
+        g.vector.wait_ge(sem["d%d" % b], 1)
+        g.vector.tensor_tensor(T.v[:, b:512:4], T.pd[:, 512 * b:512 * b + W], T.g[:, b:512:4], AluOpType.subtract).then_inc(sem.sub, 1)
+    g.vector.wait_ge(sem.sub, 4)
+    myc, mys = T["c%d" % rank], T["s%d" % rank]
+    g.vector.quantize_mx(myc[:], mys[:], T.v[:]).then_inc(sem.vq, 1)
+    g.vector.wait_ge(sem.ldx, 16)
+    g.vector.quantize_mx(T.xc[:], T.xs[:], T.xt[:]).then_inc(sem.xq, 1)
+
+    hop = way[rank]
+    sent = 0
+    g.wait_ge(sem.vq, 1)
+    call = []
+    for piece in (CODES_A, CODES_B):
+        es = first_mask(topo, core, hop[piece], piece)
+        sent += len(es)
+        call.append(RemoteDMATransfer(dst_ids=[to(topo, hop[piece], core)], dma_engine_mask=bits(es), remote_sem=sem.rin,
+                                      srcs=[view(T, rank, piece)], dsts=[view(T, rank, piece)]))
+    g.remote_dma_fused(call, local_sem=sem.sent)
+    es = first_mask(topo, core, hop[PLANE], PLANE)
+    rid, pid = topo.addr(hop[PLANE], core)
+    g.remote_dma(mys[:], mys[:], sem.rin, sem.sent, pid, rid, bits(es))
+    sent += len(es)
+    es = near_mask(topo, core, T.cores[mate], hop[PLANE])
+    rid, pid = topo.addr(T.cores[mate], core)
+    whole = view(T, rank, "codes")
+    g.remote_dma(whole, whole, sem["arr%d" % rank], sem.sent, pid, rid, bits(es))
+    g.remote_dma(mys[:], mys[:], sem["arr%d" % rank], sem.sent, pid, rid, bits(es))
+    sent += 2 * len(es)
+    g.wait_ge(sem.sent, sent)
+
+    g.tensor.wait_ge(sem.vq, 1)
+    g.tensor.wait_ge(sem.xq, 1)
+    g.tensor.matmul_mx(T.py[:, 0:NC], myc[:], mys[:], T.xc[:], T.xs[:], True, True).then_inc(sem.m0, 1)
+    g.tensor.wait_ge(sem["arr%d" % mate], 2 * len(near_mask(topo, T.cores[mate], core, way[mate][PLANE])))
+    g.tensor.matmul_mx(T.py[:, 512:512 + NC], T["c%d" % mate][:], T["s%d" % mate][:], T.xc[:], T.xs[:], True, True).then_inc(sem.m1, 1)
+    for i, j in enumerate(away):
+        n = sum(len(engines(topo, way[j][p], core)) for p in (CODES_A, CODES_B, PLANE))
+        g.tensor.wait_ge(sem["arr%d" % j], n)
+        bank = (T.py, 1024) if i == 0 else (T.pd, 0)
+        for h in range(2):
+            at = bank[1] + 512 * h
+            g.tensor.matmul_mx(bank[0][:, at:at + W], T["c%d" % j][:], T["s%d" % j][:], T.xc[:, W * h:W * h + W], T.xs[:, W * h:W * h + W],
+                               True, True).then_inc(sem["mn"[h] + "%d" % (2 + i)], 1)
+
+    def out(j, a=0, b=NC):
+        return T.o[:, NC * j + a:NC * j + b]
+
+    g.vector.wait_ge(sem.m0, 1)
+    g.vector.tensor_copy(out(rank), T.py[:, 0:NC]).then_inc(sem.k0, 1)
+    g.scalar.wait_ge(sem.m1, 1)
+    g.scalar.activation(out(mate), T.py[:, 512:512 + NC], ActivationFunctionType.Copy).then_inc(sem.k1, 1)
+    for i, j in enumerate(away):
+        buf, at = (T.py, 1024) if i == 0 else (T.pd, 0)
+        g.vector.wait_ge(sem["m%d" % (2 + i)], 1)
+        g.vector.tensor_copy(out(j, 0, W), buf[:, at:at + W]).then_inc(sem["k%d" % (2 + i)], 1)
+        g.scalar.wait_ge(sem["n%d" % (2 + i)], 1)
+        g.scalar.activation(out(j, W, NC), buf[:, at + 512:at + 512 + W], ActivationFunctionType.Copy).then_inc(sem["l%d" % (2 + i)], 1)
+
+    for k, j in (("k0", rank), ("k1", mate)):
+        g.sync.wait_ge(sem[k], 1)
+        g.sync.dma_start(T.y[:, NC * j:NC * j + NC], out(j)).then_inc(sem.st, 16)
+    for q, i, s in ((g.sync, 2, "st"), (g.scalar, 3, "sz")):
+        j = away[i - 2]
+        q.wait_ge(sem["k%d" % i], 1)
+        q.wait_ge(sem["l%d" % i], 1)
+        q.dma_start(T.y[:, NC * j:NC * j + NC], out(j)).then_inc(sem[s], 16)
+    g.sync.wait_ge(sem.st, 48)
+    g.scalar.wait_ge(sem.sz, 16)
+
+
+def first_mask(topo, src, relay, piece):
+    es = engines(topo, src, relay)
+    return {CODES_A: es[0::2], CODES_B: es[1::2], PLANE: es}[piece]
+
+
+def near_mask(topo, src, dst, relay):
+    off = engines(topo, src, relay)
+    return [e for e in engines(topo, src, dst) if e not in off]

@@ -2,11 +2,19 @@ from concourse.bass import DstId, RemoteDMATransfer
 from concourse.mybir import dt, AluOpType, ActivationFunctionType
 
 N, NC, W = 4, 256, 128
-HOSTS, PER_HOST, PER_CHIP = 4, 128, 8
+HOSTS, PER_HOST = 4, 128
+STEP = 2.0 ** -4
+
+ALL, EVEN, ODD = (0, 1), (0, 2), (1, 2)
+LO, HI, CODES, PLANE = ("c", 0, 64), ("c", 64, 128), ("c", 0, 128), ("s", 0, 128)
+CALLS = [[(LO, "A", EVEN), (HI, "B", ODD)], [(PLANE, "R", ALL)]]
+FORWARD = {"A": [(LO, "same", EVEN), (LO, "other", ODD)], "B": [(HI, "same", EVEN), (HI, "other", ODD)],
+           "R": [(PLANE, "same", EVEN), (PLANE, "other", ODD)]}
+PLACE = {"A": ("cable", 1), "B": ("switch", 0), "R": ("switch", 3)}
 
 SCRATCH = {
     "e": ("sbuf", [128, 516], "bfloat16"),
-    "one": ("sbuf", [128, 128], "bfloat16"),
+    "sq": ("sbuf", [128, 128], "bfloat16"),
     "g": ("sbuf", [128, 512], "bfloat16"),
     "v": ("sbuf", [128, 512], "bfloat16"),
     "xt": ("sbuf", [128, 1024], "bfloat16"),
@@ -23,17 +31,14 @@ SCRATCH = {
 for _j in range(N):
     SCRATCH["c%d" % _j] = ("sbuf", [128, 128], "float8_e4m3fn_x4")
     SCRATCH["s%d" % _j] = ("sbuf", [128, 128], "uint8")
-SEMAPHORES = ["seed", "ident", "sq", "ldw", "ldg", "ldx", "gs", "d0", "d1", "d2", "d3", "sub", "vq", "xq",
-              "arr0", "arr1", "arr2", "arr3", "rin", "sent", "m0", "m1", "m2", "m3", "n2", "n3",
+SEMAPHORES = ["seed", "num", "ident", "q0", "q1", "q2", "q3", "ldw", "ldg", "ldx", "g0", "g1", "g2", "g3", "d0", "d1", "d2", "d3",
+              "sub", "vq", "xq", "arr0", "arr1", "arr2", "arr3", "rin", "sent", "m0", "m1", "m2", "m3", "n2", "n3",
               "k0", "k1", "k2", "k3", "l2", "l3", "st", "sz"]
 
-CODES_A, CODES_B, PLANE = "codes_a", "codes_b", "plane"
-SPLIT = 64
 
-
-def engines(topo, src, dst):
+def engines(topo, src, dst, part=ALL):
     m = topo.mask(src, dst)
-    return [i for i in range(16) if (m >> i) & 1]
+    return [i for i in range(16) if (m >> i) & 1][part[0]::part[1]]
 
 
 def bits(es):
@@ -50,19 +55,47 @@ def near(topo, a, b):
 
 
 def relays(topo, src, dst):
-    cable, switch = [], []
+    ways = {"cable": [], "switch": []}
     for c in range(HOSTS * PER_HOST):
         if (topo.host(c) not in (topo.host(src), topo.host(dst)) and topo.chip(c) == topo.chip(src)
                 and topo.die(c) == topo.die(src) and topo.may_write(src, c) and topo.may_write(c, dst)):
-            (switch if topo.rack(topo.host(c)) == topo.rack(topo.host(src)) else cable).append(c)
-    return {CODES_A: cable[1], CODES_B: switch[0], PLANE: switch[-1]}
+            ways["switch" if topo.rack(topo.host(c)) == topo.rack(topo.host(src)) else "cable"].append(c)
+    return {k: ways[w][i] for k, (w, i) in PLACE.items()}
+
+
+def target(topo, src, far, which):
+    return [d for d in far if (topo.die(d) == topo.die(src)) == (which == "same")][0]
 
 
 def view(T, j, piece):
-    if piece == PLANE:
-        return T["s%d" % j][:]
-    a, b = {CODES_A: (0, SPLIT), CODES_B: (SPLIT, W)}.get(piece, (0, W))
+    kind, a, b = piece
+    if kind == "s":
+        return T["s%d" % j][:, a:b]
     return T["c%d" % j][:, a:b].bitcast(dt.uint8)
+
+
+def near_mask(topo, src, dst, relay):
+    off = engines(topo, src, relay)
+    return [e for e in engines(topo, src, dst) if e not in off]
+
+
+def forward(g, core, T, topo, far, way):
+    sem = T.sem
+    for j, src in enumerate(T.cores):
+        for tag, r in way[j].items():
+            if r != core:
+                continue
+            came = [part for call in CALLS for (p, t, part) in call if t == tag][0]
+            g.wait_ge(sem.rin, len(engines(topo, src, core, came)))
+            total = 0
+            for piece, which, part in FORWARD[tag]:
+                d = target(topo, src, far[j], which)
+                es = engines(topo, core, d, part)
+                rid, pid = topo.addr(d, core)
+                v = view(T, j, piece)
+                g.remote_dma(v, v, sem["arr%d" % j], sem.sent, pid, rid, bits(es))
+                total += len(es)
+            g.wait_ge(sem.sent, total)
 
 
 def rank_program(g, core, T, topo):
@@ -70,48 +103,41 @@ def rank_program(g, core, T, topo):
     sem = T.sem
     far = {j: [d for d in T.cores if not near(topo, d, c)] for j, c in enumerate(T.cores)}
     way = {j: relays(topo, c, far[j][0]) for j, c in enumerate(T.cores)}
-
     if rank is None:
-        for j in range(N):
-            for piece in (CODES_A, CODES_B, PLANE):
-                if way[j][piece] == core:
-                    src = T.cores[j]
-                    es = engines(topo, core, far[j][0])
-                    g.wait_ge(sem.rin, len(first_mask(topo, src, core, piece)))
-                    v = view(T, j, piece)
-                    g.remote_dma_fused([RemoteDMATransfer(dst_ids=[to(topo, d, core) for d in far[j]], dma_engine_mask=bits(es),
-                                                          remote_sem=sem["arr%d" % j], srcs=[v], dsts=[v for d in far[j]])],
-                                       local_sem=sem.sent)
-                    g.wait_ge(sem.sent, len(es))
+        forward(g, core, T, topo, far, way)
         return
 
     mate = [j for j, c in enumerate(T.cores) if c != core and near(topo, c, core)][0]
-    away = [j for j, c in enumerate(T.cores) if not near(topo, c, core)]
+    away = [T.cores.index(target(topo, core, far[rank], which)) for which in ("same", "other")]
 
     g.sync.dma_start(T.lc[:].bitcast(dt.uint8), T.wc[:]).then_inc(sem.ldw, 16)
-    g.sync.dma_start(T.ls[:], T.ws[:]).then_inc(sem.ldw, 16)
+    g.scalar.dma_start(T.ls[:], T.ws[:]).then_inc(sem.ldw, 16)
     g.scalar.dma_start(T.g[:], T.gr[:]).then_inc(sem.ldg, 16)
     g.scalar.dma_start(T.xt[:], T.x[:]).then_inc(sem.ldx, 16)
 
+    g.iota(T.sq[:], [[1, 128]], 0, -1, allow_small_or_imprecise_dtypes=True).then_inc(sem.num, 1)
     g.vector.memset(T.e[:], 0.0).then_inc(sem.seed, 1)
-    g.vector.memset(T.one[:], 1.0).then_inc(sem.seed, 1)
-    g.wait_ge(sem.seed, 2)
-    g.affine_select(T.e[:, 3:515:4], T.one[:], [[-1, 128]], AluOpType.is_equal, 0.0, 0, 1).then_inc(sem.ident, 1)
+    g.vector.wait_ge(sem.seed, 1)
+    g.vector.wait_ge(sem.num, 1)
+    g.vector.tensor_scalar(T.e[:, 3:515:4], T.sq[:], 0.0, None, AluOpType.is_equal).then_inc(sem.ident, 1)
     g.vector.wait_ge(sem.ident, 1)
     for b in range(4):
-        g.vector.quantize_mx(T.kc[:, W * b:W * b + W], T.ks[:, W * b:W * b + W], T.e[:, 3 - b:515 - b]).then_inc(sem.sq, 1)
-    g.vector.wait_ge(sem.ldg, 16)
-    g.vector.tensor_scalar(T.g[:], T.g[:], 2.0 ** -4, None, AluOpType.mult).then_inc(sem.gs, 1)
+        g.vector.quantize_mx(T.kc[:, W * b:W * b + W], T.ks[:, W * b:W * b + W], T.e[:, 3 - b:515 - b]).then_inc(sem["q%d" % b], 1)
 
-    g.tensor.wait_ge(sem.sq, 4)
     g.tensor.wait_ge(sem.ldw, 32)
     for b in range(4):
+        g.tensor.wait_ge(sem["q%d" % b], 1)
         g.tensor.matmul_mx(T.pd[:, 512 * b:512 * b + W], T.kc[:, W * b:W * b + W], T.ks[:, W * b:W * b + W], T.lc[:], T.ls[:],
                            True, True).then_inc(sem["d%d" % b], 1)
 
-    g.vector.wait_ge(sem.gs, 1)
+    g.vector.wait_ge(sem.ldg, 16)
+    g.vector.tensor_scalar(T.g[:, 0:512:4], T.g[:, 0:512:4], STEP, None, AluOpType.mult).then_inc(sem.g0, 1)
+    g.scalar.wait_ge(sem.ldg, 16)
+    for b in range(1, 4):
+        g.scalar.activation(T.g[:, b:512:4], T.g[:, b:512:4], ActivationFunctionType.Copy, scale=STEP).then_inc(sem["g%d" % b], 1)
     for b in range(4):
         g.vector.wait_ge(sem["d%d" % b], 1)
+        g.vector.wait_ge(sem["g%d" % b], 1)
         g.vector.tensor_tensor(T.v[:, b:512:4], T.pd[:, 512 * b:512 * b + W], T.g[:, b:512:4], AluOpType.subtract).then_inc(sem.sub, 1)
     g.vector.wait_ge(sem.sub, 4)
     myc, mys = T["c%d" % rank], T["s%d" % rank]
@@ -122,38 +148,35 @@ def rank_program(g, core, T, topo):
     hop = way[rank]
     sent = 0
     g.wait_ge(sem.vq, 1)
-    call = []
-    for piece in (CODES_A, CODES_B):
-        es = first_mask(topo, core, hop[piece], piece)
-        sent += len(es)
-        call.append(RemoteDMATransfer(dst_ids=[to(topo, hop[piece], core)], dma_engine_mask=bits(es), remote_sem=sem.rin,
-                                      srcs=[view(T, rank, piece)], dsts=[view(T, rank, piece)]))
-    g.remote_dma_fused(call, local_sem=sem.sent)
-    es = first_mask(topo, core, hop[PLANE], PLANE)
-    rid, pid = topo.addr(hop[PLANE], core)
-    g.remote_dma(mys[:], mys[:], sem.rin, sem.sent, pid, rid, bits(es))
-    sent += len(es)
-    es = near_mask(topo, core, T.cores[mate], hop[PLANE])
+    for call in CALLS:
+        ts = []
+        for piece, tag, part in call:
+            es = engines(topo, core, hop[tag], part)
+            sent += len(es)
+            ts.append(RemoteDMATransfer(dst_ids=[to(topo, hop[tag], core)], dma_engine_mask=bits(es), remote_sem=sem.rin,
+                                        srcs=[view(T, rank, piece)], dsts=[view(T, rank, piece)]))
+        g.remote_dma_fused(ts, local_sem=sem.sent)
+    es = near_mask(topo, core, T.cores[mate], hop["A"])
     rid, pid = topo.addr(T.cores[mate], core)
-    whole = view(T, rank, "codes")
-    g.remote_dma(whole, whole, sem["arr%d" % rank], sem.sent, pid, rid, bits(es))
-    g.remote_dma(mys[:], mys[:], sem["arr%d" % rank], sem.sent, pid, rid, bits(es))
-    sent += 2 * len(es)
+    for piece in (CODES, PLANE):
+        g.remote_dma(view(T, rank, piece), view(T, rank, piece), sem["arr%d" % rank], sem.sent, pid, rid, bits(es))
+        sent += len(es)
     g.wait_ge(sem.sent, sent)
 
     g.tensor.wait_ge(sem.vq, 1)
     g.tensor.wait_ge(sem.xq, 1)
     g.tensor.matmul_mx(T.py[:, 0:NC], myc[:], mys[:], T.xc[:], T.xs[:], True, True).then_inc(sem.m0, 1)
-    g.tensor.wait_ge(sem["arr%d" % mate], 2 * len(near_mask(topo, T.cores[mate], core, way[mate][PLANE])))
+    g.tensor.wait_ge(sem["arr%d" % mate], 2 * len(near_mask(topo, T.cores[mate], core, way[mate]["A"])))
     g.tensor.matmul_mx(T.py[:, 512:512 + NC], T["c%d" % mate][:], T["s%d" % mate][:], T.xc[:], T.xs[:], True, True).then_inc(sem.m1, 1)
+    banks = [(T.py, 1024), (T.pd, 0)]
     for i, j in enumerate(away):
-        n = sum(len(engines(topo, way[j][p], core)) for p in (CODES_A, CODES_B, PLANE))
+        n = sum(len(engines(topo, way[j][tag], core, part)) for tag in FORWARD for (p, which, part) in FORWARD[tag]
+                if target(topo, T.cores[j], far[j], which) == core)
         g.tensor.wait_ge(sem["arr%d" % j], n)
-        bank = (T.py, 1024) if i == 0 else (T.pd, 0)
         for h in range(2):
-            at = bank[1] + 512 * h
-            g.tensor.matmul_mx(bank[0][:, at:at + W], T["c%d" % j][:], T["s%d" % j][:], T.xc[:, W * h:W * h + W], T.xs[:, W * h:W * h + W],
-                               True, True).then_inc(sem["mn"[h] + "%d" % (2 + i)], 1)
+            at = banks[i][1] + 512 * h
+            g.tensor.matmul_mx(banks[i][0][:, at:at + W], T["c%d" % j][:], T["s%d" % j][:], T.xc[:, W * h:W * h + W],
+                               T.xs[:, W * h:W * h + W], True, True).then_inc(sem["mn"[h] + "%d" % (2 + i)], 1)
 
     def out(j, a=0, b=NC):
         return T.o[:, NC * j + a:NC * j + b]
@@ -163,7 +186,7 @@ def rank_program(g, core, T, topo):
     g.scalar.wait_ge(sem.m1, 1)
     g.scalar.activation(out(mate), T.py[:, 512:512 + NC], ActivationFunctionType.Copy).then_inc(sem.k1, 1)
     for i, j in enumerate(away):
-        buf, at = (T.py, 1024) if i == 0 else (T.pd, 0)
+        buf, at = banks[i]
         g.vector.wait_ge(sem["m%d" % (2 + i)], 1)
         g.vector.tensor_copy(out(j, 0, W), buf[:, at:at + W]).then_inc(sem["k%d" % (2 + i)], 1)
         g.scalar.wait_ge(sem["n%d" % (2 + i)], 1)
@@ -179,13 +202,3 @@ def rank_program(g, core, T, topo):
         q.dma_start(T.y[:, NC * j:NC * j + NC], out(j)).then_inc(sem[s], 16)
     g.sync.wait_ge(sem.st, 48)
     g.scalar.wait_ge(sem.sz, 16)
-
-
-def first_mask(topo, src, relay, piece):
-    es = engines(topo, src, relay)
-    return {CODES_A: es[0::2], CODES_B: es[1::2], PLANE: es}[piece]
-
-
-def near_mask(topo, src, dst, relay):
-    off = engines(topo, src, relay)
-    return [e for e in engines(topo, src, dst) if e not in off]

@@ -1,4 +1,3 @@
-from concourse.bass import DstId, RemoteDMATransfer
 from concourse.mybir import dt, AluOpType, ActivationFunctionType
 
 N, NC, W = 4, 256, 128
@@ -6,17 +5,22 @@ HOSTS, PER_HOST = 4, 128
 STEP = 2.0 ** -4
 
 ALL, EVEN, ODD = (0, 1), (0, 2), (1, 2)
-LO, HI, CODES, PLANE = ("c", 0, 64), ("c", 64, 128), ("c", 0, 128), ("s", 0, 128)
-CALLS = [[(LO, "A", EVEN), (HI, "B", ODD)], [(PLANE, "R", ALL)]]
+CUT = 70
+PAD = 4 * (W - CUT)
+E0 = PAD + 4 * W
+V0 = W - CUT
+LO, HI, CODES, PLANE = ("c", 0, CUT), ("c", CUT, W), ("c", 0, W), ("s", 0, W)
+CALLS = [(LO, "A", EVEN), (HI, "B", ODD), (PLANE, "R", ALL)]
 FORWARD = {"A": [(LO, "same", EVEN), (LO, "other", ODD)], "B": [(HI, "same", EVEN), (HI, "other", ODD)],
            "R": [(PLANE, "same", EVEN), (PLANE, "other", ODD)]}
 PLACE = {"A": ("cable", 1), "B": ("switch", 0), "R": ("switch", 3)}
 
 SCRATCH = {
-    "e": ("sbuf", [128, 516], "bfloat16"),
-    "sq": ("sbuf", [128, 128], "bfloat16"),
+    "sq": ("sbuf", [128, 64], "bfloat16"),
     "g": ("sbuf", [128, 512], "bfloat16"),
-    "v": ("sbuf", [128, 512], "bfloat16"),
+    "v": ("sbuf", [128, E0 + 516], "bfloat16"),
+    "vc": ("sbuf", [128, 256], "float8_e4m3fn_x4"),
+    "vs": ("sbuf", [128, 256], "uint8"),
     "xt": ("sbuf", [128, 1024], "bfloat16"),
     "xc": ("sbuf", [128, 256], "float8_e4m3fn_x4"),
     "xs": ("sbuf", [128, 256], "uint8"),
@@ -31,9 +35,9 @@ SCRATCH = {
 for _j in range(N):
     SCRATCH["c%d" % _j] = ("sbuf", [128, 128], "float8_e4m3fn_x4")
     SCRATCH["s%d" % _j] = ("sbuf", [128, 128], "uint8")
-SEMAPHORES = ["seed", "num", "ident", "q0", "q1", "q2", "q3", "ldw", "ldg", "ldx", "g0", "g1", "g2", "g3", "d0", "d1", "d2", "d3",
-              "sub", "vq", "xq", "arr0", "arr1", "arr2", "arr3", "rin", "sent", "m0", "m1", "m2", "m3", "n2", "n3",
-              "k0", "k1", "k2", "k3", "l2", "l3", "st", "sz"]
+SEMAPHORES = ["seed", "pad", "num", "ident", "q0", "q1", "q2", "q3", "ldw", "lg0", "lg1", "ldx", "d0", "d1", "d2", "d3",
+              "sub0", "sub1", "v0", "v1", "xq", "arr0", "arr1", "arr2", "arr3", "rin", "gone", "sent",
+              "m0", "m1", "m2", "m3", "n2", "n3", "k0", "k1", "k2", "k3", "l2", "l3", "st", "sz"]
 
 
 def engines(topo, src, dst, part=ALL):
@@ -43,11 +47,6 @@ def engines(topo, src, dst, part=ALL):
 
 def bits(es):
     return sum(1 << i for i in es)
-
-
-def to(topo, dst, src):
-    rid, pid = topo.addr(dst, src)
-    return DstId(rid=rid, pnc=pid)
 
 
 def near(topo, a, b):
@@ -74,6 +73,13 @@ def view(T, j, piece):
     return T["c%d" % j][:, a:b].bitcast(dt.uint8)
 
 
+def made(T, piece):
+    kind, a, b = piece
+    if kind == "s":
+        return T.vs[:, V0 + a:V0 + b]
+    return T.vc[:, V0 + a:V0 + b].bitcast(dt.uint8)
+
+
 def near_mask(topo, src, dst, relay):
     off = engines(topo, src, relay)
     return [e for e in engines(topo, src, dst) if e not in off]
@@ -85,7 +91,7 @@ def forward(g, core, T, topo, far, way):
         for tag, r in way[j].items():
             if r != core:
                 continue
-            came = [part for call in CALLS for (p, t, part) in call if t == tag][0]
+            came = [part for (p, t, part) in CALLS if t == tag][0]
             g.wait_ge(sem.rin, len(engines(topo, src, core, came)))
             total = 0
             for piece, which, part in FORWARD[tag]:
@@ -109,20 +115,27 @@ def rank_program(g, core, T, topo):
 
     mate = [j for j, c in enumerate(T.cores) if c != core and near(topo, c, core)][0]
     away = [T.cores.index(target(topo, core, far[rank], which)) for which in ("same", "other")]
+    runs = ((0, CUT), (CUT, W))
 
     g.sync.dma_start(T.lc[:].bitcast(dt.uint8), T.wc[:]).then_inc(sem.ldw, 16)
     g.scalar.dma_start(T.ls[:], T.ws[:]).then_inc(sem.ldw, 16)
-    g.scalar.dma_start(T.g[:], T.gr[:]).then_inc(sem.ldg, 16)
+    for h, (a, z) in enumerate(runs):
+        g.scalar.dma_start(T.g[:, 4 * a:4 * z], T.gr[:, 4 * a:4 * z]).then_inc(sem["lg%d" % h], 16)
+    g.scalar.wait_ge(sem.lg0, 16)
     g.scalar.dma_start(T.xt[:], T.x[:]).then_inc(sem.ldx, 16)
 
-    g.iota(T.sq[:], [[1, 128]], 0, -1, allow_small_or_imprecise_dtypes=True).then_inc(sem.num, 1)
-    g.vector.memset(T.e[:], 0.0).then_inc(sem.seed, 1)
+    g.iota(T.sq[:], [[1, 64]], 0, -1, allow_small_or_imprecise_dtypes=True).then_inc(sem.num, 1)
+    g.vector.memset(T.v[:, E0:E0 + 516], 0.0).then_inc(sem.seed, 1)
     g.vector.wait_ge(sem.seed, 1)
     g.vector.wait_ge(sem.num, 1)
-    g.vector.tensor_scalar(T.e[:, 3:515:4], T.sq[:], 0.0, None, AluOpType.is_equal).then_inc(sem.ident, 1)
-    g.vector.wait_ge(sem.ident, 1)
+    for h in range(2):
+        g.vector.tensor_scalar(T.v[:, E0 + 3 + 256 * h:E0 + 259 + 256 * h:4], T.sq[:], -64.0 * h, 1.0 / STEP,
+                               AluOpType.is_equal, AluOpType.mult).then_inc(sem.ident, 1)
+    g.vector.wait_ge(sem.ident, 2)
     for b in range(4):
-        g.vector.quantize_mx(T.kc[:, W * b:W * b + W], T.ks[:, W * b:W * b + W], T.e[:, 3 - b:515 - b]).then_inc(sem["q%d" % b], 1)
+        g.vector.quantize_mx(T.kc[:, W * b:W * b + W], T.ks[:, W * b:W * b + W],
+                             T.v[:, E0 + 3 - b:E0 + 515 - b]).then_inc(sem["q%d" % b], 1)
+    g.vector.memset(T.v[:, 0:PAD], 0.0).then_inc(sem.pad, 1)
 
     g.tensor.wait_ge(sem.ldw, 32)
     for b in range(4):
@@ -130,42 +143,42 @@ def rank_program(g, core, T, topo):
         g.tensor.matmul_mx(T.pd[:, 512 * b:512 * b + W], T.kc[:, W * b:W * b + W], T.ks[:, W * b:W * b + W], T.lc[:], T.ls[:],
                            True, True).then_inc(sem["d%d" % b], 1)
 
-    g.vector.wait_ge(sem.ldg, 16)
-    g.vector.tensor_scalar(T.g[:, 0:512:4], T.g[:, 0:512:4], STEP, None, AluOpType.mult).then_inc(sem.g0, 1)
-    g.scalar.wait_ge(sem.ldg, 16)
-    for b in range(1, 4):
-        g.scalar.activation(T.g[:, b:512:4], T.g[:, b:512:4], ActivationFunctionType.Copy, scale=STEP).then_inc(sem["g%d" % b], 1)
-    for b in range(4):
-        g.vector.wait_ge(sem["d%d" % b], 1)
-        g.vector.wait_ge(sem["g%d" % b], 1)
-        g.vector.tensor_tensor(T.v[:, b:512:4], T.pd[:, 512 * b:512 * b + W], T.g[:, b:512:4], AluOpType.subtract).then_inc(sem.sub, 1)
-    g.vector.wait_ge(sem.sub, 4)
-    myc, mys = T["c%d" % rank], T["s%d" % rank]
-    g.vector.quantize_mx(myc[:], mys[:], T.v[:]).then_inc(sem.vq, 1)
+    for h, (a, z) in enumerate(runs):
+        g.vector.wait_ge(sem["lg%d" % h], 16)
+        for b in range(4):
+            if h == 0:
+                g.vector.wait_ge(sem["d%d" % b], 1)
+            g.vector.tensor_tensor(T.v[:, PAD + 4 * a + b:PAD + 4 * z:4], T.pd[:, 512 * b + a:512 * b + z], T.g[:, 4 * a + b:4 * z:4],
+                                   AluOpType.subtract).then_inc(sem["sub%d" % h], 1)
+        if h == 0:
+            g.vector.wait_ge(sem.pad, 1)
+        g.vector.wait_ge(sem["sub%d" % h], 4)
+        g.vector.quantize_mx(T.vc[:, W * h:W * h + W], T.vs[:, W * h:W * h + W], T.v[:, 512 * h:512 * h + 512]).then_inc(sem["v%d" % h], 1)
     g.vector.wait_ge(sem.ldx, 16)
     g.vector.quantize_mx(T.xc[:], T.xs[:], T.xt[:]).then_inc(sem.xq, 1)
 
     hop = way[rank]
-    sent = 0
-    g.wait_ge(sem.vq, 1)
-    for call in CALLS:
-        ts = []
-        for piece, tag, part in call:
-            es = engines(topo, core, hop[tag], part)
-            sent += len(es)
-            ts.append(RemoteDMATransfer(dst_ids=[to(topo, hop[tag], core)], dma_engine_mask=bits(es), remote_sem=sem.rin,
-                                        srcs=[view(T, rank, piece)], dsts=[view(T, rank, piece)]))
-        g.remote_dma_fused(ts, local_sem=sem.sent)
+    gone = sent = 0
+    for piece, tag, part in CALLS:
+        es = engines(topo, core, hop[tag], part)
+        rid, pid = topo.addr(hop[tag], core)
+        g.wait_ge(sem.v0, 1)
+        if piece != LO:
+            g.wait_ge(sem.v1, 1)
+        g.remote_dma(view(T, rank, piece), made(T, piece), sem.rin, sem.gone, pid, rid, bits(es))
+        gone += len(es)
     es = near_mask(topo, core, T.cores[mate], hop["A"])
     rid, pid = topo.addr(T.cores[mate], core)
     for piece in (CODES, PLANE):
-        g.remote_dma(view(T, rank, piece), view(T, rank, piece), sem["arr%d" % rank], sem.sent, pid, rid, bits(es))
+        g.remote_dma(view(T, rank, piece), made(T, piece), sem["arr%d" % rank], sem.sent, pid, rid, bits(es))
         sent += len(es)
+    g.wait_ge(sem.gone, gone)
     g.wait_ge(sem.sent, sent)
 
-    g.tensor.wait_ge(sem.vq, 1)
+    g.tensor.wait_ge(sem.v0, 1)
+    g.tensor.wait_ge(sem.v1, 1)
     g.tensor.wait_ge(sem.xq, 1)
-    g.tensor.matmul_mx(T.py[:, 0:NC], myc[:], mys[:], T.xc[:], T.xs[:], True, True).then_inc(sem.m0, 1)
+    g.tensor.matmul_mx(T.py[:, 0:NC], T.vc[:, V0:V0 + W], T.vs[:, V0:V0 + W], T.xc[:], T.xs[:], True, True).then_inc(sem.m0, 1)
     g.tensor.wait_ge(sem["arr%d" % mate], 2 * len(near_mask(topo, T.cores[mate], core, way[mate]["A"])))
     g.tensor.matmul_mx(T.py[:, 512:512 + NC], T["c%d" % mate][:], T["s%d" % mate][:], T.xc[:], T.xs[:], True, True).then_inc(sem.m1, 1)
     banks = [(T.py, 1024), (T.pd, 0)]
@@ -182,23 +195,24 @@ def rank_program(g, core, T, topo):
         return T.o[:, NC * j + a:NC * j + b]
 
     g.vector.wait_ge(sem.m0, 1)
-    g.vector.tensor_copy(out(rank), T.py[:, 0:NC]).then_inc(sem.k0, 1)
+    g.vector.tensor_scalar(out(rank), T.py[:, 0:NC], STEP, None, AluOpType.mult).then_inc(sem.k0, 1)
     g.scalar.wait_ge(sem.m1, 1)
-    g.scalar.activation(out(mate), T.py[:, 512:512 + NC], ActivationFunctionType.Copy).then_inc(sem.k1, 1)
+    g.scalar.activation(out(mate), T.py[:, 512:512 + NC], ActivationFunctionType.Copy, scale=STEP).then_inc(sem.k1, 1)
     for i, j in enumerate(away):
         buf, at = banks[i]
         g.vector.wait_ge(sem["m%d" % (2 + i)], 1)
-        g.vector.tensor_copy(out(j, 0, W), buf[:, at:at + W]).then_inc(sem["k%d" % (2 + i)], 1)
+        g.vector.tensor_scalar(out(j, 0, W), buf[:, at:at + W], STEP, None, AluOpType.mult).then_inc(sem["k%d" % (2 + i)], 1)
         g.scalar.wait_ge(sem["n%d" % (2 + i)], 1)
-        g.scalar.activation(out(j, W, NC), buf[:, at + 512:at + 512 + W], ActivationFunctionType.Copy).then_inc(sem["l%d" % (2 + i)], 1)
+        g.scalar.activation(out(j, W, NC), buf[:, at + 512:at + 512 + W], ActivationFunctionType.Copy,
+                            scale=STEP).then_inc(sem["l%d" % (2 + i)], 1)
 
-    for k, j in (("k0", rank), ("k1", mate)):
-        g.sync.wait_ge(sem[k], 1)
-        g.sync.dma_start(T.y[:, NC * j:NC * j + NC], out(j)).then_inc(sem.st, 16)
-    for q, i, s in ((g.sync, 2, "st"), (g.scalar, 3, "sz")):
-        j = away[i - 2]
-        q.wait_ge(sem["k%d" % i], 1)
-        q.wait_ge(sem["l%d" % i], 1)
-        q.dma_start(T.y[:, NC * j:NC * j + NC], out(j)).then_inc(sem[s], 16)
-    g.sync.wait_ge(sem.st, 48)
+    g.sync.wait_ge(sem.gone, gone)
+    first, last = away
+    for ks, j, b in ((("k0",), rank, NC), (("k1",), mate, NC), (("k2", "l2"), first, NC), (("k3",), last, W)):
+        for k in ks:
+            g.sync.wait_ge(sem[k], 1)
+        g.sync.dma_start(T.y[:, NC * j:NC * j + b], out(j, 0, b)).then_inc(sem.st, 16)
+    g.scalar.wait_ge(sem.l3, 1)
+    g.scalar.dma_start(T.y[:, NC * last + W:NC * last + NC], out(last, W, NC)).then_inc(sem.sz, 16)
+    g.sync.wait_ge(sem.st, 64)
     g.scalar.wait_ge(sem.sz, 16)

from concourse.mybir import dt, AluOpType, ActivationFunctionType

N, NC, W = 4, 256, 128
HOSTS, PER_HOST = 4, 128
STEP = 2.0 ** -4

ALL, EVEN, ODD = (0, 1), (0, 2), (1, 2)
CUT = 70
PAD = 4 * (W - CUT)
E0 = PAD + 4 * W
V0 = W - CUT
LO, HI, CODES, PLANE = ("c", 0, CUT), ("c", CUT, W), ("c", 0, W), ("s", 0, W)
CALLS = [(LO, "A", EVEN), (HI, "B", ODD), (PLANE, "R", ALL)]
FORWARD = {"A": [(LO, "same", EVEN), (LO, "other", ODD)], "B": [(HI, "same", EVEN), (HI, "other", ODD)],
           "R": [(PLANE, "same", EVEN), (PLANE, "other", ODD)]}
PLACE = {"A": ("cable", 1), "B": ("switch", 0), "R": ("switch", 3)}

SCRATCH = {
    "sq": ("sbuf", [128, 64], "bfloat16"),
    "g": ("sbuf", [128, 512], "bfloat16"),
    "v": ("sbuf", [128, E0 + 516], "bfloat16"),
    "vc": ("sbuf", [128, 256], "float8_e4m3fn_x4"),
    "vs": ("sbuf", [128, 256], "uint8"),
    "xt": ("sbuf", [128, 1024], "bfloat16"),
    "xc": ("sbuf", [128, 256], "float8_e4m3fn_x4"),
    "xs": ("sbuf", [128, 256], "uint8"),
    "kc": ("sbuf", [128, 512], "float8_e4m3fn_x4"),
    "ks": ("sbuf", [128, 512], "uint8"),
    "lc": ("sbuf", [128, 128], "float8_e4m3fn_x4"),
    "ls": ("sbuf", [128, 128], "uint8"),
    "o": ("sbuf", [128, N * NC], "float32"),
    "pd": ("psum", [128, 2048], "float32"),
    "py": ("psum", [128, 2048], "float32"),
}
for _j in range(N):
    SCRATCH["c%d" % _j] = ("sbuf", [128, 128], "float8_e4m3fn_x4")
    SCRATCH["s%d" % _j] = ("sbuf", [128, 128], "uint8")
SEMAPHORES = ["seed", "pad", "num", "ident", "q0", "q1", "q2", "q3", "ldw", "lg0", "lg1", "ldx", "d0", "d1", "d2", "d3",
              "sub0", "sub1", "v0", "v1", "xq", "arr0", "arr1", "arr2", "arr3", "rin", "gone", "sent",
              "m0", "m1", "m2", "m3", "n2", "n3", "k0", "k1", "k2", "k3", "l2", "l3", "st", "sz"]


def engines(topo, src, dst, part=ALL):
    m = topo.mask(src, dst)
    return [i for i in range(16) if (m >> i) & 1][part[0]::part[1]]


def bits(es):
    return sum(1 << i for i in es)


def near(topo, a, b):
    return topo.host(a) == topo.host(b) and topo.chip(a) == topo.chip(b)


def relays(topo, src, dst):
    ways = {"cable": [], "switch": []}
    for c in range(HOSTS * PER_HOST):
        if (topo.host(c) not in (topo.host(src), topo.host(dst)) and topo.chip(c) == topo.chip(src)
                and topo.die(c) == topo.die(src) and topo.may_write(src, c) and topo.may_write(c, dst)):
            ways["switch" if topo.rack(topo.host(c)) == topo.rack(topo.host(src)) else "cable"].append(c)
    return {k: ways[w][i] for k, (w, i) in PLACE.items()}


def target(topo, src, far, which):
    return [d for d in far if (topo.die(d) == topo.die(src)) == (which == "same")][0]


def view(T, j, piece):
    kind, a, b = piece
    if kind == "s":
        return T["s%d" % j][:, a:b]
    return T["c%d" % j][:, a:b].bitcast(dt.uint8)


def made(T, piece):
    kind, a, b = piece
    if kind == "s":
        return T.vs[:, V0 + a:V0 + b]
    return T.vc[:, V0 + a:V0 + b].bitcast(dt.uint8)


def near_mask(topo, src, dst, relay):
    off = engines(topo, src, relay)
    return [e for e in engines(topo, src, dst) if e not in off]


def forward(g, core, T, topo, far, way):
    sem = T.sem
    for j, src in enumerate(T.cores):
        for tag, r in way[j].items():
            if r != core:
                continue
            came = [part for (p, t, part) in CALLS if t == tag][0]
            g.wait_ge(sem.rin, len(engines(topo, src, core, came)))
            total = 0
            for piece, which, part in FORWARD[tag]:
                d = target(topo, src, far[j], which)
                es = engines(topo, core, d, part)
                rid, pid = topo.addr(d, core)
                v = view(T, j, piece)
                g.remote_dma(v, v, sem["arr%d" % j], sem.sent, pid, rid, bits(es))
                total += len(es)
            g.wait_ge(sem.sent, total)


def rank_program(g, core, T, topo):
    rank = T.rank_of(core)
    sem = T.sem
    far = {j: [d for d in T.cores if not near(topo, d, c)] for j, c in enumerate(T.cores)}
    way = {j: relays(topo, c, far[j][0]) for j, c in enumerate(T.cores)}
    if rank is None:
        forward(g, core, T, topo, far, way)
        return

    mate = [j for j, c in enumerate(T.cores) if c != core and near(topo, c, core)][0]
    away = [T.cores.index(target(topo, core, far[rank], which)) for which in ("same", "other")]
    runs = ((0, CUT), (CUT, W))

    g.sync.dma_start(T.lc[:].bitcast(dt.uint8), T.wc[:]).then_inc(sem.ldw, 16)
    g.scalar.dma_start(T.ls[:], T.ws[:]).then_inc(sem.ldw, 16)
    for h, (a, z) in enumerate(runs):
        g.scalar.dma_start(T.g[:, 4 * a:4 * z], T.gr[:, 4 * a:4 * z]).then_inc(sem["lg%d" % h], 16)
    g.scalar.wait_ge(sem.lg0, 16)
    g.scalar.dma_start(T.xt[:], T.x[:]).then_inc(sem.ldx, 16)

    g.iota(T.sq[:], [[1, 64]], 0, -1, allow_small_or_imprecise_dtypes=True).then_inc(sem.num, 1)
    g.vector.memset(T.v[:, E0:E0 + 516], 0.0).then_inc(sem.seed, 1)
    g.vector.wait_ge(sem.seed, 1)
    g.vector.wait_ge(sem.num, 1)
    for h in range(2):
        g.vector.tensor_scalar(T.v[:, E0 + 3 + 256 * h:E0 + 259 + 256 * h:4], T.sq[:], -64.0 * h, 1.0 / STEP,
                               AluOpType.is_equal, AluOpType.mult).then_inc(sem.ident, 1)
    g.vector.wait_ge(sem.ident, 2)
    for b in range(4):
        g.vector.quantize_mx(T.kc[:, W * b:W * b + W], T.ks[:, W * b:W * b + W],
                             T.v[:, E0 + 3 - b:E0 + 515 - b]).then_inc(sem["q%d" % b], 1)
    g.vector.memset(T.v[:, 0:PAD], 0.0).then_inc(sem.pad, 1)

    g.tensor.wait_ge(sem.ldw, 32)
    for b in range(4):
        g.tensor.wait_ge(sem["q%d" % b], 1)
        g.tensor.matmul_mx(T.pd[:, 512 * b:512 * b + W], T.kc[:, W * b:W * b + W], T.ks[:, W * b:W * b + W], T.lc[:], T.ls[:],
                           True, True).then_inc(sem["d%d" % b], 1)

    for h, (a, z) in enumerate(runs):
        g.vector.wait_ge(sem["lg%d" % h], 16)
        for b in range(4):
            if h == 0:
                g.vector.wait_ge(sem["d%d" % b], 1)
            g.vector.tensor_tensor(T.v[:, PAD + 4 * a + b:PAD + 4 * z:4], T.pd[:, 512 * b + a:512 * b + z], T.g[:, 4 * a + b:4 * z:4],
                                   AluOpType.subtract).then_inc(sem["sub%d" % h], 1)
        if h == 0:
            g.vector.wait_ge(sem.pad, 1)
        g.vector.wait_ge(sem["sub%d" % h], 4)
        g.vector.quantize_mx(T.vc[:, W * h:W * h + W], T.vs[:, W * h:W * h + W], T.v[:, 512 * h:512 * h + 512]).then_inc(sem["v%d" % h], 1)
    g.vector.wait_ge(sem.ldx, 16)
    g.vector.quantize_mx(T.xc[:], T.xs[:], T.xt[:]).then_inc(sem.xq, 1)

    hop = way[rank]
    gone = sent = 0
    for piece, tag, part in CALLS:
        es = engines(topo, core, hop[tag], part)
        rid, pid = topo.addr(hop[tag], core)
        g.wait_ge(sem.v0, 1)
        if piece != LO:
            g.wait_ge(sem.v1, 1)
        g.remote_dma(view(T, rank, piece), made(T, piece), sem.rin, sem.gone, pid, rid, bits(es))
        gone += len(es)
    es = near_mask(topo, core, T.cores[mate], hop["A"])
    rid, pid = topo.addr(T.cores[mate], core)
    for piece in (CODES, PLANE):
        g.remote_dma(view(T, rank, piece), made(T, piece), sem["arr%d" % rank], sem.sent, pid, rid, bits(es))
        sent += len(es)
    g.wait_ge(sem.gone, gone)
    g.wait_ge(sem.sent, sent)

    g.tensor.wait_ge(sem.v0, 1)
    g.tensor.wait_ge(sem.v1, 1)
    g.tensor.wait_ge(sem.xq, 1)
    g.tensor.matmul_mx(T.py[:, 0:NC], T.vc[:, V0:V0 + W], T.vs[:, V0:V0 + W], T.xc[:], T.xs[:], True, True).then_inc(sem.m0, 1)
    g.tensor.wait_ge(sem["arr%d" % mate], 2 * len(near_mask(topo, T.cores[mate], core, way[mate]["A"])))
    g.tensor.matmul_mx(T.py[:, 512:512 + NC], T["c%d" % mate][:], T["s%d" % mate][:], T.xc[:], T.xs[:], True, True).then_inc(sem.m1, 1)
    banks = [(T.py, 1024), (T.pd, 0)]
    for i, j in enumerate(away):
        n = sum(len(engines(topo, way[j][tag], core, part)) for tag in FORWARD for (p, which, part) in FORWARD[tag]
                if target(topo, T.cores[j], far[j], which) == core)
        g.tensor.wait_ge(sem["arr%d" % j], n)
        for h in range(2):
            at = banks[i][1] + 512 * h
            g.tensor.matmul_mx(banks[i][0][:, at:at + W], T["c%d" % j][:], T["s%d" % j][:], T.xc[:, W * h:W * h + W],
                               T.xs[:, W * h:W * h + W], True, True).then_inc(sem["mn"[h] + "%d" % (2 + i)], 1)

    def out(j, a=0, b=NC):
        return T.o[:, NC * j + a:NC * j + b]

    g.vector.wait_ge(sem.m0, 1)
    g.vector.tensor_scalar(out(rank), T.py[:, 0:NC], STEP, None, AluOpType.mult).then_inc(sem.k0, 1)
    g.scalar.wait_ge(sem.m1, 1)
    g.scalar.activation(out(mate), T.py[:, 512:512 + NC], ActivationFunctionType.Copy, scale=STEP).then_inc(sem.k1, 1)
    for i, j in enumerate(away):
        buf, at = banks[i]
        g.vector.wait_ge(sem["m%d" % (2 + i)], 1)
        g.vector.tensor_scalar(out(j, 0, W), buf[:, at:at + W], STEP, None, AluOpType.mult).then_inc(sem["k%d" % (2 + i)], 1)
        g.scalar.wait_ge(sem["n%d" % (2 + i)], 1)
        g.scalar.activation(out(j, W, NC), buf[:, at + 512:at + 512 + W], ActivationFunctionType.Copy,
                            scale=STEP).then_inc(sem["l%d" % (2 + i)], 1)

    g.sync.wait_ge(sem.gone, gone)
    first, last = away
    for ks, j, b in ((("k0",), rank, NC), (("k1",), mate, NC), (("k2", "l2"), first, NC), (("k3",), last, W)):
        for k in ks:
            g.sync.wait_ge(sem[k], 1)
        g.sync.dma_start(T.y[:, NC * j:NC * j + b], out(j, 0, b)).then_inc(sem.st, 16)
    g.scalar.wait_ge(sem.l3, 1)
    g.scalar.dma_start(T.y[:, NC * last + W:NC * last + NC], out(last, W, NC)).then_inc(sem.sz, 16)
    g.sync.wait_ge(sem.st, 64)
    g.scalar.wait_ge(sem.sz, 16)
